import numpy as np
import ml_dtypes


def mxq(x, axis, fmt="e4m3"):
    dtype, down = {"e4m3": (ml_dtypes.float8_e4m3fn, 7), "e5m2": (ml_dtypes.float8_e5m2, 14)}[fmt]
    v = np.moveaxis(np.asarray(x, np.float32).astype(ml_dtypes.bfloat16).astype(np.float64), axis, -1)
    blocks = v.reshape(v.shape[:-1] + (-1, 32))
    amax = np.abs(blocks).max(-1, keepdims=True)
    byte = np.maximum(np.where(amax > 0, np.frexp(amax)[1] - 1 + 127, 0) - down, 1)
    scale = np.exp2(byte - 127.0)
    codes = (blocks / scale).astype(np.float32).astype(dtype).astype(np.float64)
    return np.moveaxis((codes * scale).reshape(v.shape), -1, axis)


WIDE = False


def mx_kscale(k):
    if not WIDE:
        return np.ones(k)
    levels = np.array([10, -10, 5, -5, 0])
    if k % 512:
        return np.exp2(np.random.permutation(np.resize(levels, k // 32))).repeat(32)
    a = np.empty((k // 512, 16))
    for p in range(k // 512):
        a[p, :8] = np.random.permutation(np.resize(levels, 8))
        for g in range(8):
            far = levels[np.abs(levels - a[p, g]) >= 10]
            a[p, g + 8] = far[np.random.randint(len(far))]
    return np.exp2(a.ravel()).repeat(32)


def f64(x):
    return np.asarray(x).astype(np.float64)


def striped(idx):
    return np.tile(np.asarray(idx).reshape(-1, 16).T, (8, 1)).astype(np.uint16)


def unstriped(offs):
    return offs[:16].T.reshape(-1).astype(np.int64)


E2M1 = np.array([0.0, 0.5, 1.0, 1.5, 2.0, 3.0, 4.0, 6.0, -0.0, -0.5, -1.0, -1.5, -2.0, -3.0, -4.0, -6.0])


def pack_weight(w, fmt):
    k, n = w.shape
    w = f64(np.asarray(w, np.float32).astype(ml_dtypes.bfloat16)).reshape(k // 32, 32, n)
    amax = np.abs(w).max(1)
    if fmt == "e4m3":
        byte = np.frexp(amax)[1] - 1 + 127 - 7
    else:
        mant, ex = np.frexp(amax / 6.0)
        byte = np.where(mant > 0.5, ex, ex - 1) + 127
    byte = np.clip(np.where(amax > 0, byte, 1), 1, 254)
    scaled = (w * np.exp2(127.0 - byte)[:, None, :]).reshape(k, n).astype(np.float32)
    by_word = np.ascontiguousarray(scaled.reshape(k // 512, 128, 4, n).transpose(0, 1, 3, 2))
    if fmt == "e4m3":
        words = by_word.astype(ml_dtypes.float8_e4m3fn).view(np.uint8)
    else:
        c = by_word.astype(ml_dtypes.float4_e2m1fn).view(np.uint8) & 0xF
        words = (c[..., 0::2] | (c[..., 1::2] << 4)).reshape(k // 512, 128, 2 * n)
    return np.ascontiguousarray(words), np.ascontiguousarray(byte.astype(np.uint8).reshape(k // 512, 16, n))


def unpack_weight(words, scales, fmt):
    g, _, n = scales.shape
    words = np.ascontiguousarray(words).reshape(g, 128, n, -1)
    if fmt == "e4m3":
        vals = words.view(ml_dtypes.float8_e4m3fn).astype(np.float64)
    else:
        nib = np.empty((g, 128, n, 4), np.uint8)
        nib[..., 0::2] = words & 0xF
        nib[..., 1::2] = words >> 4
        vals = E2M1[nib]
    vals = vals * np.repeat(np.exp2(scales.astype(np.float64) - 127.0), 8, axis=1)[..., None]
    return vals.transpose(0, 1, 3, 2).reshape(g * 512, n)


D, K, R, T, I, Q, G = 512, 512, 512, 2048, 512, 128, 32


def setup_inputs():
    n = np.random.standard_normal
    idx = np.random.permutation(T)[:I]
    fd = mx_kscale(D)
    fk = mx_kscale(K)
    fr = mx_kscale(R)
    keysp = pack_weight(n((D, T)) / fd[:, None], "e4m3")
    tabp = pack_weight(n((K, T)) / fk[:, None], "e4m3")
    return {
        "query": (n((D, Q)) * 0.7 / np.sqrt(D) * fd[:, None]).astype(np.float32),
        "keys_words": keysp[0],
        "keys_scales": keysp[1],
        "tab_words": tabp[0],
        "tab_scales": tabp[1],
        "w1": (n((K, R)) * 1 / np.sqrt(K) * fk[:, None]).astype(np.float32),
        "share": (np.random.uniform(0.4, 1.0, (R, 1))).astype(np.float32),
        "gout": (n((R, Q)) * 1 / np.sqrt(R) * fr[:, None]).astype(np.float32),
        "hsc": (np.random.uniform(0.7, 1.4, (R, 1)) / fr[:, None]).astype(np.float32),
        "old": (0.5 * n((Q, T))).astype(np.float32),
        "offs": striped(idx),
    }


def reference(query, keys_words, keys_scales, tab_words, tab_scales, w1, share, gout, hsc, old, offs):
    idx = unstriped(offs)
    keysu = unpack_weight(keys_words, keys_scales, "e4m3")
    tabu = unpack_weight(tab_words, tab_scales, "e4m3")
    queryq = mxq(f64(query), 0, "e4m3")
    keysidxg = keysu[:, idx]
    a = queryq.T @ keysidxg
    p = np.exp(a - np.max(a, axis=1, keepdims=True))
    z = np.sum(p, axis=1, keepdims=True)
    w1q = mxq(f64(w1), 0, "e4m3")
    tabidxg = tabu[:, idx]
    zh = w1q.T @ tabidxg
    mz = zh.reshape(R, G, I // G).mean(axis=2)
    mzr = np.repeat(mz, I // G, axis=1)
    hv = np.tanh(zh - mzr * f64(share))
    hs1 = hv * f64(hsc)
    goutq = mxq(f64(gout), 0, "e4m3")
    hs1q = mxq(hs1, 0, "e4m3")
    c0 = goutq.T @ hs1q
    dz = np.sum(c0 * p / np.square(z) * (-1.0), axis=1, keepdims=True)
    dp = c0 / z + dz
    da = dp * p
    gs = da * 512.0
    gf = np.zeros((Q, T))
    gf[:, idx] = gs
    y = f64(old) + gf
    return y

@@ -1,0 +1,199 @@
+from contextlib import ExitStack
+
+import concourse.mybir as mybir
+
+D, K, R, T, I, Q = 512, 512, 512, 2048, 512, 128
+PAGE = 16
+FLOPS = 2 * (D * Q * I + K * R * I + R * Q * I)
+
+F32 = mybir.dt.float32
+BF16 = mybir.dt.bfloat16
+I32 = mybir.dt.int32
+U32 = mybir.dt.uint32
+U16 = mybir.dt.uint16
+U8 = mybir.dt.uint8
+FP8X4 = mybir.dt.float8_e4m3fn_x4
+ALU = mybir.AluOpType
+ACT = mybir.ActivationFunctionType
+AX = mybir.AxisListType
+
+P = 128
+PACK = 4
+CHUNK = 128
+CHUNKS = I // CHUNK
+PAGES = CHUNK // PAGE
+SCALAR_CHUNKS = 3
+OUT_PARTS = [256, 512, 512, 512, 256]
+
+
+def tile_attend_blrcentred_soft_kernel(tc, query, keys_words, keys_scales, tab_words, tab_scales, w1, share, gout, hsc, old, offs, out):
+    nc = tc.nc
+    with ExitStack() as ctx:
+        sb = ctx.enter_context(tc.tile_pool(name="sb", bufs=1))
+        ps = ctx.enter_context(tc.psum_pool(name="ps", bufs=1))
+
+        def tile(name, shape, dtype):
+            return sb.tile(shape, dtype, name=name, align_bytes=64)
+
+        offsets = tile("offsets", [P, I // 16], U16)
+        nc.sync.dma_start(offsets[:], offs)
+
+        tab_s = tile("tab_s", [P, T], U8)
+        keys_s = tile("keys_s", [P, T], U8)
+        window = tile("window", [P, T], F32)
+        consts = tile("consts", [P, 2], F32)
+        zero = tile("zero", [P, 1], F32)
+        warm = tile("warm", [P, 1], F32)
+        nc.vector.memset(tab_s[:].bitcast(I32), 0)
+        nc.vector.memset(keys_s[:].bitcast(I32), 0)
+        nc.vector.memset(zero[:], 0.0)
+        nc.scalar.activation(warm[:], zero[:], ACT.Exp)
+        keys_plane = tile("keys_plane", [P, I], U8)
+        nc.vector.memset(keys_plane[:].bitcast(I32), 0)
+
+        nc.vector.memset(window[:], 0.0)
+        nc.vector.memset(consts[:, 0:1], 512.0)
+        nc.vector.memset(consts[:, 1:2], -1.0)
+
+        halves = 2
+        half_cols = R // halves
+        w_raw = [tile("w_raw%d" % h, [P, PACK, half_cols], F32) for h in range(halves)]
+        w_rows = w1.rearrange("(p j) c -> p j c", j=PACK)
+
+        def load_scales(plane, rows):
+            for quad in range(4):
+                nc.sync.dma_start(plane[32 * quad:32 * quad + 4, :].bitcast(I32), rows[0, 4 * quad:4 * quad + 4, :].bitcast(I32))
+
+        nc.sync.dma_start(w_raw[0][:], w_rows[:, :, :half_cols])
+        load_scales(tab_s, tab_scales)
+        nc.sync.dma_start(keys_s[0:16, :].bitcast(I32), keys_scales[0].bitcast(I32))
+        nc.sync.dma_start(w_raw[1][:], w_rows[:, :, half_cols:])
+        tab_w = tile("tab_w", [P, T], U32)
+        nc.sync.dma_start(tab_w[:].bitcast(I32), tab_words[0].rearrange("p n t -> p (n t)").bitcast(I32))
+        share_t = tile("share_t", [P, PACK], F32)
+        hsc_t = tile("hsc_t", [P, PACK], F32)
+        nc.sync.dma_start(share_t[:], share.rearrange("(p t) o -> p (t o)", t=PACK))
+        nc.sync.dma_start(hsc_t[:], hsc.rearrange("(p t) o -> p (t o)", t=PACK))
+        keys_w = tile("keys_w", [P, T], U32)
+        q_raw = tile("q_raw", [P, PACK, Q], F32)
+        g_raw = tile("g_raw", [P, PACK, Q], F32)
+        nc.sync.dma_start(g_raw[:], gout.rearrange("(p j) c -> p j c", j=PACK))
+        nc.sync.dma_start(q_raw[:], query.rearrange("(p j) c -> p j c", j=PACK))
+        tab_sg = tile("tab_sg", [P, I], U8)
+        nc.vector.tensor_copy(tab_sg[:], tab_s[:].indirect(offsets[:]))
+        keys_sg = tile("keys_sg", [P, I], U8)
+        nc.vector.tensor_copy(keys_sg[:], keys_s[:].indirect(offsets[:]))
+        for quad in range(4):
+            nc.sync.dma_start(keys_plane[32 * quad:32 * quad + 4, :].bitcast(I32), keys_sg[4 * quad:4 * quad + 4, :].bitcast(I32))
+        nc.sync.dma_start(keys_w[:].bitcast(I32), keys_words[0].rearrange("p n t -> p (n t)").bitcast(I32))
+        old_t = tile("old_t", [P, T], F32)
+        nc.sync.dma_start(old_t[:], old)
+
+
+        w_grp = tile("w_grp", [P, PACK * P * PACK], BF16)
+        w_codes = tile("w_codes", [P, R], U32)
+        w_scales = tile("w_scales", [P, R], U8)
+        w_view = w_grp[:].rearrange("p (t m j) -> p m j t", t=PACK, j=PACK)
+        half_m = P // halves
+        nc.scalar.copy(w_view[:, :half_m], w_raw[0][:].rearrange("p j (m t) -> p m j t", t=PACK))
+        nc.vector.tensor_copy(w_view[:, half_m:], w_raw[1][:].rearrange("p j (m t) -> p m j t", t=PACK))
+        nc.vector.quantize_mx(out=w_codes[:].bitcast(FP8X4), scales=w_scales[:], in_=w_grp[:])
+
+        neg_share = tile("neg_share", [P, PACK], F32)
+        nc.vector.tensor_scalar(neg_share[:], share_t[:], -1.0 / PAGE, None, ALU.mult)
+
+        tab_g = tile("tab_g", [P, I], U32)
+        for h in range(2):
+            nc.vector.tensor_copy(tab_g[:, 256 * h:256 * (h + 1)], tab_w[:].indirect(offsets[:, 16 * h:16 * (h + 1)]))
+
+        def interleave(dst, src):
+            nc.scalar.copy(dst.rearrange("p (c i t) -> p c t i", i=4, t=PACK), src.rearrange("p t (c i) -> p c t i", i=4))
+
+        def quantize(name, grouped):
+            codes = tile(name + "_codes", [P, P], U32)
+            scales = tile(name + "_scales", [P, P], U8)
+            nc.vector.quantize_mx(out=codes[:].bitcast(FP8X4), scales=scales[:], in_=grouped)
+            return codes, scales
+
+        c0_bank = ps.tile([P, I], F32, name="c0_bank")
+        zh_banks = [ps.tile([P, PACK, CHUNK], F32, name="zh%d" % c) for c in range(CHUNKS)]
+        hs_grp = [tile("hs_grp%d" % c, [P, CHUNK * PACK], BF16) for c in range(CHUNKS)]
+
+        def layer(c):
+            cols = slice(c * CHUNK, (c + 1) * CHUNK)
+            bank = zh_banks[c]
+            for t in range(PACK):
+                nc.tensor.matmul_mx(out=bank[:, t, :], lhsT=w_codes[:, t * P:(t + 1) * P].bitcast(FP8X4), lhsT_scale=w_scales[:, t * P:(t + 1) * P],
+                                    rhs=tab_g[:, cols].bitcast(FP8X4), rhs_scale=tab_sg[:, cols], start=True, stop=True)
+            sums = tile("sums%d" % c, [P, PAGES, PACK], F32)
+            nc.vector.tensor_reduce(sums[:].rearrange("p g t -> p t g"), bank[:].rearrange("p t (g j) -> p t g j", j=PAGE), AX.X, ALU.add)
+            x = tile("x%d" % c, [P, PACK * CHUNK], F32)
+            hv = tile("hv%d" % c, [P, PACK * CHUNK], F32)
+            if c < SCALAR_CHUNKS:
+                for t in range(PACK):
+                    nc.vector.scalar_tensor_tensor(
+                        x[:, t * CHUNK:(t + 1) * CHUNK].rearrange("p (g j) -> p g j", j=PAGE),
+                        sums[:, :, t:t + 1].to_broadcast([P, PAGES, PAGE]), neg_share[:, t:t + 1],
+                        bank[:, t, :].rearrange("p (g j) -> p g j", j=PAGE), ALU.mult, ALU.add)
+                nc.scalar.activation(hv[:], x[:], ACT.Tanh)
+                hs = tile("hs%d" % c, [P, PACK, CHUNK], BF16)
+                for t in range(PACK):
+                    nc.scalar.activation(hs[:, t, :], hv[:, t * CHUNK:(t + 1) * CHUNK], ACT.Copy, scale=hsc_t[:, t:t + 1])
+                interleave(hs_grp[c][:], hs[:])
+            else:
+                shift = tile("shift%d" % c, [P, PAGES, PACK], F32)
+                nc.vector.tensor_tensor(shift[:], sums[:], neg_share[:].unsqueeze(1).to_broadcast([P, PAGES, PACK]), ALU.mult)
+                nc.vector.tensor_tensor(x[:].rearrange("p (g j t) -> p g j t", j=PAGE, t=PACK), bank[:].rearrange("p t (g j) -> p g j t", j=PAGE),
+                                        shift[:].unsqueeze(2).to_broadcast([P, PAGES, PAGE, PACK]), ALU.add)
+                nc.scalar.activation(hv[:], x[:], ACT.Tanh)
+                nc.vector.tensor_tensor(hs_grp[c][:].rearrange("p (i t) -> p i t", t=PACK), hv[:].rearrange("p (i t) -> p i t", t=PACK),
+                                        hsc_t[:].unsqueeze(1).to_broadcast([P, CHUNK, PACK]), ALU.mult)
+
+        def read_back(c):
+            codes, scales = quantize("hs%d" % c, hs_grp[c][:])
+            nc.tensor.matmul_mx(out=c0_bank[:, c * CHUNK:(c + 1) * CHUNK], lhsT=g_codes[:].bitcast(FP8X4), lhsT_scale=g_scales[:],
+                                rhs=codes[:].bitcast(FP8X4), rhs_scale=scales[:], start=True, stop=True)
+
+        g_grp = tile("g_grp", [P, Q * PACK], BF16)
+        interleave(g_grp[:], g_raw[:])
+        q_grp = tile("q_grp", [P, Q * PACK], BF16)
+        interleave(q_grp[:], q_raw[:])
+        layer(0)
+        layer(1)
+        layer(2)
+        g_codes, g_scales = quantize("g", g_grp[:])
+        read_back(0)
+        keys_g = tile("keys_g", [P, I], U32)
+        nc.vector.tensor_copy(keys_g[:], keys_w[:].indirect(offsets[:]))
+        q_codes, q_scales = quantize("q", q_grp[:])
+        score_bank = ps.tile([P, I], F32, name="score_bank")
+        nc.tensor.matmul_mx(out=score_bank[:], lhsT=q_codes[:].bitcast(FP8X4), lhsT_scale=q_scales[:],
+                            rhs=keys_g[:].bitcast(FP8X4), rhs_scale=keys_plane[:], start=True, stop=True)
+        read_back(1)
+        layer(3)
+        neg_max = tile("neg_max", [P, 1], F32)
+        nc.vector.tensor_reduce(neg_max[:], score_bank[:], AX.X, ALU.max, negate=True)
+        p = tile("p", [P, I], F32)
+        z = tile("z", [P, 1], F32)
+        nc.scalar.activation(p[:], score_bank[:], ACT.Exp, bias=neg_max[:], accum_out=z[:])
+        read_back(2)
+        rz = tile("rz", [P, 1], F32)
+        nc.vector.reciprocal(rz[:], z[:])
+        factors = tile("factors", [P, 2], F32)
+        nc.vector.tensor_scalar(factors[:], consts[:], rz[:], None, ALU.mult)
+        read_back(3)
+
+        cw = tile("cw", [P, I], F32)
+        total = tile("total", [P, 1], F32)
+        nc.vector.scalar_tensor_tensor(cw[:], c0_bank[:], factors[:, 0:1], p[:], ALU.mult, ALU.mult, accum_out=total[:])
+        pull = tile("pull", [P, I], F32)
+        nc.vector.tensor_scalar(pull[:], p[:], total[:], factors[:, 1:2], ALU.mult, ALU.mult)
+        nc.vector.tensor_tensor(window[:].indirect(offsets[:]), cw[:], pull[:], ALU.add)
+
+        start = 0
+        for n, width in enumerate(OUT_PARTS):
+            cols = slice(start, start + width)
+            res = tile("res%d" % n, [P, width], F32)
+            nc.vector.tensor_tensor(res[:], old_t[:, cols], window[:, cols], ALU.add)
+            nc.sync.dma_start(out[:, cols], res[:])
+            start = start + width

@@ -96,7 +96,7 @@ def tile_attend_blrcentred_soft_kernel(tc, query, keys_words, keys_scales, tab_w
         w_view = w_grp[:].rearrange("p (t m j) -> p m j t", t=PACK, j=PACK)
         half_m = P // halves
         nc.scalar.copy(w_view[:, :half_m], w_raw[0][:].rearrange("p j (m t) -> p m j t", t=PACK))
-        nc.vector.tensor_copy(w_view[:, half_m:], w_raw[1][:].rearrange("p j (m t) -> p m j t", t=PACK))
+        nc.scalar.copy(w_view[:, half_m:], w_raw[1][:].rearrange("p j (m t) -> p m j t", t=PACK))
         nc.vector.quantize_mx(out=w_codes[:].bitcast(FP8X4), scales=w_scales[:], in_=w_grp[:])
 
         neg_share = tile("neg_share", [P, PACK], F32)
@@ -160,28 +160,26 @@ def tile_attend_blrcentred_soft_kernel(tc, query, keys_words, keys_scales, tab_w
         interleave(q_grp[:], q_raw[:])
         layer(0)
         layer(1)
-        layer(2)
-        g_codes, g_scales = quantize("g", g_grp[:])
-        read_back(0)
         keys_g = tile("keys_g", [P, I], U32)
         nc.vector.tensor_copy(keys_g[:], keys_w[:].indirect(offsets[:]))
         q_codes, q_scales = quantize("q", q_grp[:])
         score_bank = ps.tile([P, I], F32, name="score_bank")
         nc.tensor.matmul_mx(out=score_bank[:], lhsT=q_codes[:].bitcast(FP8X4), lhsT_scale=q_scales[:],
                             rhs=keys_g[:].bitcast(FP8X4), rhs_scale=keys_plane[:], start=True, stop=True)
-        read_back(1)
-        layer(3)
+        layer(2)
         neg_max = tile("neg_max", [P, 1], F32)
         nc.vector.tensor_reduce(neg_max[:], score_bank[:], AX.X, ALU.max, negate=True)
+        layer(3)
         p = tile("p", [P, I], F32)
         z = tile("z", [P, 1], F32)
         nc.scalar.activation(p[:], score_bank[:], ACT.Exp, bias=neg_max[:], accum_out=z[:])
-        read_back(2)
+        g_codes, g_scales = quantize("g", g_grp[:])
+        for c in range(CHUNKS):
+            read_back(c)
         rz = tile("rz", [P, 1], F32)
         nc.vector.reciprocal(rz[:], z[:])
         factors = tile("factors", [P, 2], F32)
         nc.vector.tensor_scalar(factors[:], consts[:], rz[:], None, ALU.mult)
-        read_back(3)
 
         cw = tile("cw", [P, I], F32)
         total = tile("total", [P, 1], F32)

@@ -42,12 +42,8 @@ def tile_attend_blrcentred_soft_kernel(tc, query, keys_words, keys_scales, tab_w
         keys_s = tile("keys_s", [P, T], U8)
         window = tile("window", [P, T], F32)
         consts = tile("consts", [P, 2], F32)
-        zero = tile("zero", [P, 1], F32)
-        warm = tile("warm", [P, 1], F32)
         nc.vector.memset(tab_s[:].bitcast(I32), 0)
         nc.vector.memset(keys_s[:].bitcast(I32), 0)
-        nc.vector.memset(zero[:], 0.0)
-        nc.scalar.activation(warm[:], zero[:], ACT.Exp)
         keys_plane = tile("keys_plane", [P, I], U8)
         nc.vector.memset(keys_plane[:].bitcast(I32), 0)
 

from contextlib import ExitStack

import concourse.mybir as mybir

D, K, R, T, I, Q = 512, 512, 512, 2048, 512, 128
PAGE = 16
FLOPS = 2 * (D * Q * I + K * R * I + R * Q * I)

F32 = mybir.dt.float32
BF16 = mybir.dt.bfloat16
I32 = mybir.dt.int32
U32 = mybir.dt.uint32
U16 = mybir.dt.uint16
U8 = mybir.dt.uint8
FP8X4 = mybir.dt.float8_e4m3fn_x4
ALU = mybir.AluOpType
ACT = mybir.ActivationFunctionType
AX = mybir.AxisListType

P = 128
PACK = 4
CHUNK = 128
CHUNKS = I // CHUNK
PAGES = CHUNK // PAGE
SCALAR_CHUNKS = 3
OUT_PARTS = [256, 512, 512, 512, 256]


def tile_attend_blrcentred_soft_kernel(tc, query, keys_words, keys_scales, tab_words, tab_scales, w1, share, gout, hsc, old, offs, out):
    nc = tc.nc
    with ExitStack() as ctx:
        sb = ctx.enter_context(tc.tile_pool(name="sb", bufs=1))
        ps = ctx.enter_context(tc.psum_pool(name="ps", bufs=1))

        def tile(name, shape, dtype):
            return sb.tile(shape, dtype, name=name, align_bytes=64)

        offsets = tile("offsets", [P, I // 16], U16)
        nc.sync.dma_start(offsets[:], offs)

        tab_s = tile("tab_s", [P, T], U8)
        keys_s = tile("keys_s", [P, T], U8)
        window = tile("window", [P, T], F32)
        consts = tile("consts", [P, 2], F32)
        nc.vector.memset(tab_s[:].bitcast(I32), 0)
        nc.vector.memset(keys_s[:].bitcast(I32), 0)
        keys_plane = tile("keys_plane", [P, I], U8)
        nc.vector.memset(keys_plane[:].bitcast(I32), 0)

        nc.vector.memset(window[:], 0.0)
        nc.vector.memset(consts[:, 0:1], 512.0)
        nc.vector.memset(consts[:, 1:2], -1.0)

        halves = 2
        half_cols = R // halves
        w_raw = [tile("w_raw%d" % h, [P, PACK, half_cols], F32) for h in range(halves)]
        w_rows = w1.rearrange("(p j) c -> p j c", j=PACK)

        def load_scales(plane, rows):
            for quad in range(4):
                nc.sync.dma_start(plane[32 * quad:32 * quad + 4, :].bitcast(I32), rows[0, 4 * quad:4 * quad + 4, :].bitcast(I32))

        nc.sync.dma_start(w_raw[0][:], w_rows[:, :, :half_cols])
        load_scales(tab_s, tab_scales)
        nc.sync.dma_start(keys_s[0:16, :].bitcast(I32), keys_scales[0].bitcast(I32))
        nc.sync.dma_start(w_raw[1][:], w_rows[:, :, half_cols:])
        tab_w = tile("tab_w", [P, T], U32)
        nc.sync.dma_start(tab_w[:].bitcast(I32), tab_words[0].rearrange("p n t -> p (n t)").bitcast(I32))
        share_t = tile("share_t", [P, PACK], F32)
        hsc_t = tile("hsc_t", [P, PACK], F32)
        nc.sync.dma_start(share_t[:], share.rearrange("(p t) o -> p (t o)", t=PACK))
        nc.sync.dma_start(hsc_t[:], hsc.rearrange("(p t) o -> p (t o)", t=PACK))
        keys_w = tile("keys_w", [P, T], U32)
        q_raw = tile("q_raw", [P, PACK, Q], F32)
        g_raw = tile("g_raw", [P, PACK, Q], F32)
        nc.sync.dma_start(g_raw[:], gout.rearrange("(p j) c -> p j c", j=PACK))
        nc.sync.dma_start(q_raw[:], query.rearrange("(p j) c -> p j c", j=PACK))
        tab_sg = tile("tab_sg", [P, I], U8)
        nc.vector.tensor_copy(tab_sg[:], tab_s[:].indirect(offsets[:]))
        keys_sg = tile("keys_sg", [P, I], U8)
        nc.vector.tensor_copy(keys_sg[:], keys_s[:].indirect(offsets[:]))
        for quad in range(4):
            nc.sync.dma_start(keys_plane[32 * quad:32 * quad + 4, :].bitcast(I32), keys_sg[4 * quad:4 * quad + 4, :].bitcast(I32))
        nc.sync.dma_start(keys_w[:].bitcast(I32), keys_words[0].rearrange("p n t -> p (n t)").bitcast(I32))
        old_t = tile("old_t", [P, T], F32)
        nc.sync.dma_start(old_t[:], old)


        w_grp = tile("w_grp", [P, PACK * P * PACK], BF16)
        w_codes = tile("w_codes", [P, R], U32)
        w_scales = tile("w_scales", [P, R], U8)
        w_view = w_grp[:].rearrange("p (t m j) -> p m j t", t=PACK, j=PACK)
        half_m = P // halves
        nc.scalar.copy(w_view[:, :half_m], w_raw[0][:].rearrange("p j (m t) -> p m j t", t=PACK))
        nc.scalar.copy(w_view[:, half_m:], w_raw[1][:].rearrange("p j (m t) -> p m j t", t=PACK))
        nc.vector.quantize_mx(out=w_codes[:].bitcast(FP8X4), scales=w_scales[:], in_=w_grp[:])

        neg_share = tile("neg_share", [P, PACK], F32)
        nc.vector.tensor_scalar(neg_share[:], share_t[:], -1.0 / PAGE, None, ALU.mult)

        tab_g = tile("tab_g", [P, I], U32)
        for h in range(2):
            nc.vector.tensor_copy(tab_g[:, 256 * h:256 * (h + 1)], tab_w[:].indirect(offsets[:, 16 * h:16 * (h + 1)]))

        def interleave(dst, src):
            nc.scalar.copy(dst.rearrange("p (c i t) -> p c t i", i=4, t=PACK), src.rearrange("p t (c i) -> p c t i", i=4))

        def quantize(name, grouped):
            codes = tile(name + "_codes", [P, P], U32)
            scales = tile(name + "_scales", [P, P], U8)
            nc.vector.quantize_mx(out=codes[:].bitcast(FP8X4), scales=scales[:], in_=grouped)
            return codes, scales

        c0_bank = ps.tile([P, I], F32, name="c0_bank")
        zh_banks = [ps.tile([P, PACK, CHUNK], F32, name="zh%d" % c) for c in range(CHUNKS)]
        hs_grp = [tile("hs_grp%d" % c, [P, CHUNK * PACK], BF16) for c in range(CHUNKS)]

        def layer(c):
            cols = slice(c * CHUNK, (c + 1) * CHUNK)
            bank = zh_banks[c]
            for t in range(PACK):
                nc.tensor.matmul_mx(out=bank[:, t, :], lhsT=w_codes[:, t * P:(t + 1) * P].bitcast(FP8X4), lhsT_scale=w_scales[:, t * P:(t + 1) * P],
                                    rhs=tab_g[:, cols].bitcast(FP8X4), rhs_scale=tab_sg[:, cols], start=True, stop=True)
            sums = tile("sums%d" % c, [P, PAGES, PACK], F32)
            nc.vector.tensor_reduce(sums[:].rearrange("p g t -> p t g"), bank[:].rearrange("p t (g j) -> p t g j", j=PAGE), AX.X, ALU.add)
            x = tile("x%d" % c, [P, PACK * CHUNK], F32)
            hv = tile("hv%d" % c, [P, PACK * CHUNK], F32)
            if c < SCALAR_CHUNKS:
                for t in range(PACK):
                    nc.vector.scalar_tensor_tensor(
                        x[:, t * CHUNK:(t + 1) * CHUNK].rearrange("p (g j) -> p g j", j=PAGE),
                        sums[:, :, t:t + 1].to_broadcast([P, PAGES, PAGE]), neg_share[:, t:t + 1],
                        bank[:, t, :].rearrange("p (g j) -> p g j", j=PAGE), ALU.mult, ALU.add)
                nc.scalar.activation(hv[:], x[:], ACT.Tanh)
                hs = tile("hs%d" % c, [P, PACK, CHUNK], BF16)
                for t in range(PACK):
                    nc.scalar.activation(hs[:, t, :], hv[:, t * CHUNK:(t + 1) * CHUNK], ACT.Copy, scale=hsc_t[:, t:t + 1])
                interleave(hs_grp[c][:], hs[:])
            else:
                shift = tile("shift%d" % c, [P, PAGES, PACK], F32)
                nc.vector.tensor_tensor(shift[:], sums[:], neg_share[:].unsqueeze(1).to_broadcast([P, PAGES, PACK]), ALU.mult)
                nc.vector.tensor_tensor(x[:].rearrange("p (g j t) -> p g j t", j=PAGE, t=PACK), bank[:].rearrange("p t (g j) -> p g j t", j=PAGE),
                                        shift[:].unsqueeze(2).to_broadcast([P, PAGES, PAGE, PACK]), ALU.add)
                nc.scalar.activation(hv[:], x[:], ACT.Tanh)
                nc.vector.tensor_tensor(hs_grp[c][:].rearrange("p (i t) -> p i t", t=PACK), hv[:].rearrange("p (i t) -> p i t", t=PACK),
                                        hsc_t[:].unsqueeze(1).to_broadcast([P, CHUNK, PACK]), ALU.mult)

        def read_back(c):
            codes, scales = quantize("hs%d" % c, hs_grp[c][:])
            nc.tensor.matmul_mx(out=c0_bank[:, c * CHUNK:(c + 1) * CHUNK], lhsT=g_codes[:].bitcast(FP8X4), lhsT_scale=g_scales[:],
                                rhs=codes[:].bitcast(FP8X4), rhs_scale=scales[:], start=True, stop=True)

        g_grp = tile("g_grp", [P, Q * PACK], BF16)
        interleave(g_grp[:], g_raw[:])
        q_grp = tile("q_grp", [P, Q * PACK], BF16)
        interleave(q_grp[:], q_raw[:])
        layer(0)
        layer(1)
        keys_g = tile("keys_g", [P, I], U32)
        nc.vector.tensor_copy(keys_g[:], keys_w[:].indirect(offsets[:]))
        q_codes, q_scales = quantize("q", q_grp[:])
        score_bank = ps.tile([P, I], F32, name="score_bank")
        nc.tensor.matmul_mx(out=score_bank[:], lhsT=q_codes[:].bitcast(FP8X4), lhsT_scale=q_scales[:],
                            rhs=keys_g[:].bitcast(FP8X4), rhs_scale=keys_plane[:], start=True, stop=True)
        layer(2)
        neg_max = tile("neg_max", [P, 1], F32)
        nc.vector.tensor_reduce(neg_max[:], score_bank[:], AX.X, ALU.max, negate=True)
        layer(3)
        p = tile("p", [P, I], F32)
        z = tile("z", [P, 1], F32)
        nc.scalar.activation(p[:], score_bank[:], ACT.Exp, bias=neg_max[:], accum_out=z[:])
        g_codes, g_scales = quantize("g", g_grp[:])
        for c in range(CHUNKS):
            read_back(c)
        rz = tile("rz", [P, 1], F32)
        nc.vector.reciprocal(rz[:], z[:])
        factors = tile("factors", [P, 2], F32)
        nc.vector.tensor_scalar(factors[:], consts[:], rz[:], None, ALU.mult)

        cw = tile("cw", [P, I], F32)
        total = tile("total", [P, 1], F32)
        nc.vector.scalar_tensor_tensor(cw[:], c0_bank[:], factors[:, 0:1], p[:], ALU.mult, ALU.mult, accum_out=total[:])
        pull = tile("pull", [P, I], F32)
        nc.vector.tensor_scalar(pull[:], p[:], total[:], factors[:, 1:2], ALU.mult, ALU.mult)
        nc.vector.tensor_tensor(window[:].indirect(offsets[:]), cw[:], pull[:], ALU.add)

        start = 0
        for n, width in enumerate(OUT_PARTS):
            cols = slice(start, start + width)
            res = tile("res%d" % n, [P, width], F32)
            nc.vector.tensor_tensor(res[:], old_t[:, cols], window[:, cols], ALU.add)
            nc.sync.dma_start(out[:, cols], res[:])
            start = start + width
